import numpy as np
import ml_dtypes


def mxq(x, axis, fmt="e4m3"):
    dtype, down = {"e4m3": (ml_dtypes.float8_e4m3fn, 7), "e5m2": (ml_dtypes.float8_e5m2, 14)}[fmt]
    v = np.moveaxis(np.asarray(x, np.float32).astype(ml_dtypes.bfloat16).astype(np.float64), axis, -1)
    blocks = v.reshape(v.shape[:-1] + (-1, 32))
    amax = np.abs(blocks).max(-1, keepdims=True)
    byte = np.maximum(np.where(amax > 0, np.frexp(amax)[1] - 1 + 127, 0) - down, 1)
    scale = np.exp2(byte - 127.0)
    codes = (blocks / scale).astype(np.float32).astype(dtype).astype(np.float64)
    return np.moveaxis((codes * scale).reshape(v.shape), -1, axis)


WIDE = False


def mx_kscale(k):
    if not WIDE:
        return np.ones(k)
    levels = np.array([10, -10, 5, -5, 0])
    if k % 512:
        return np.exp2(np.random.permutation(np.resize(levels, k // 32))).repeat(32)
    a = np.empty((k // 512, 16))
    for p in range(k // 512):
        a[p, :8] = np.random.permutation(np.resize(levels, 8))
        for g in range(8):
            far = levels[np.abs(levels - a[p, g]) >= 10]
            a[p, g + 8] = far[np.random.randint(len(far))]
    return np.exp2(a.ravel()).repeat(32)


def f64(x):
    return np.asarray(x).astype(np.float64)


def striped(idx):
    return np.tile(idx.reshape(-1, 16).T, (8, 1)).astype(np.uint16)


def unstriped(offs):
    return offs[:16].T.reshape(-1).astype(np.int64)


def pack_weight(w):
    k, n = w.shape
    w = f64(np.asarray(w, np.float32).astype(ml_dtypes.bfloat16)).reshape(k // 32, 32, n)
    amax = np.abs(w).max(1)
    byte = np.clip(np.where(amax > 0, np.frexp(amax)[1] - 1 + 127 - 7, 1), 1, 254)
    scaled = (w * np.exp2(127.0 - byte)[:, None, :]).reshape(k, n).astype(np.float32)
    words = np.ascontiguousarray(scaled.reshape(k // 512, 128, 4, n).transpose(0, 1, 3, 2)).astype(ml_dtypes.float8_e4m3fn).view(np.uint8)
    return words, np.ascontiguousarray(byte.astype(np.uint8).reshape(k // 512, 16, n))


def unpack_weight(words, scales):
    g, p, n, _ = words.shape
    vals = np.ascontiguousarray(words).view(ml_dtypes.float8_e4m3fn).astype(np.float64) * np.repeat(np.exp2(scales.astype(np.float64) - 127.0), 8, axis=1)[..., None]
    return vals.transpose(0, 1, 3, 2).reshape(g * 512, n)


K, T, S, N, H, W = 512, 2048, 512, 128, 512, 1024


def setup_inputs():
    n = np.random.standard_normal
    s = mx_kscale(K)[:, None]
    u = mx_kscale(H)
    packed_xT = pack_weight(n((K, T)) * s)
    packed_eT = pack_weight(n((K, W)) * s)
    return {
        "x_words": packed_xT[0],
        "x_scales": packed_xT[1],
        "w1": (n((K, H)) / np.sqrt(K) / s).astype(np.float32),
        "e_words": packed_eT[0],
        "e_scales": packed_eT[1],
        "w2": (n((K, H)) / np.sqrt(K) / s).astype(np.float32),
        "unit": (np.random.uniform(0.6, 1.4, (H, 1)) * u[:, None]).astype(np.float32),
        "w3": (n((H, N)) / np.sqrt(H) / u[:, None]).astype(np.float32),
        "offs": striped(np.random.permutation(T)[:S]),
        "mds": striped(np.random.permutation(W)[:S]),
        "md": striped(np.random.permutation(S)),
        "prv": striped(np.random.permutation(S)),
    }


def reference(x_words, x_scales, w1, e_words, e_scales, w2, unit, w3, offs, mds, md, prv):
    xq = unpack_weight(x_words, x_scales)[:, unstriped(offs)]
    y = mxq(f64(w1), 0, "e4m3").T @ xq
    e_mds = unpack_weight(e_words, e_scales)[:, unstriped(mds)]
    ye = mxq(f64(w2), 0, "e4m3").T @ e_mds
    em = ye[:, unstriped(md)]
    res1 = y * em
    rp = res1[:, unstriped(prv)]
    acc2 = res1 + rp
    hid = f64(unit) * (acc2 * em)
    return mxq(f64(w3), 0, "e4m3").T @ mxq(hid, 0, "e4m3")

@@ -1,0 +1,173 @@
+from contextlib import ExitStack
+
+import concourse.mybir as mybir
+
+K, T, S, N, H, W = 512, 2048, 512, 128, 512, 1024
+FLOPS = 2 * K * H * S * 2 + 2 * H * N * S
+
+F32 = mybir.dt.float32
+BF16 = mybir.dt.bfloat16
+I32 = mybir.dt.int32
+U32 = mybir.dt.uint32
+U16 = mybir.dt.uint16
+U8 = mybir.dt.uint8
+FP8X4 = mybir.dt.float8_e4m3fn_x4
+MULT = mybir.AluOpType.mult
+ADD = mybir.AluOpType.add
+COPY = mybir.ActivationFunctionType.Copy
+
+P = 128
+PACK = 4
+STRIPE = 16
+HALF = S // 2
+CHUNKS = ((0, 128), (128, 256), (256, 384), (384, 512))
+
+
+def tile_picked_ytransc_acc_p_kernel(tc, x_words, x_scales, w1, e_words, e_scales, w2, unit, w3, offs, mds, md, prv, out):
+    nc = tc.nc
+    with ExitStack() as ctx:
+        keep = ctx.enter_context(tc.tile_pool(name="keep", bufs=1))
+        psum = ctx.enter_context(tc.psum_pool(name="psum", bufs=1))
+
+        def load_list(src, name):
+            lst = keep.tile([P, S // STRIPE], U16, name=name)
+            nc.sync.dma_start(lst[:], src)
+            return lst
+
+        def load_words(src, cols, name):
+            words = keep.tile([P, cols], I32, name=name, align_bytes=64)
+            nc.sync.dma_start(words[:], src[0].rearrange("p n t -> p (n t)").bitcast(I32))
+            return words
+
+        def clear_scales(cols, name):
+            scales = keep.tile([P, cols], U8, name=name, align_bytes=64)
+            nc.vector.memset(scales[:].bitcast(I32), 0)
+            return scales
+
+        def load_scales(queue, scales, src):
+            for q in range(4):
+                queue.dma_start(scales[32 * q : 32 * q + 4, :].bitcast(I32), src[0, 4 * q : 4 * q + 4, :].bitcast(I32))
+
+        def load_weight(src, c0, c1, name):
+            raw = keep.tile([P, PACK, c1 - c0], F32, name=name)
+            nc.sync.dma_start(raw[:], src.rearrange("(p j) c -> p j c", j=PACK)[:, :, c0:c1])
+            return raw
+
+        def pick(table, lst, dtype, name, tag):
+            picked = keep.tile([P, S], dtype, name=name, tag=tag, align_bytes=64)
+            nc.vector.tensor_copy(picked[:], table[:].bitcast(dtype).indirect(lst[:]))
+            return picked
+
+        def deal(copy, grouped, raw, c0, c1):
+            dst = grouped[:].rearrange("p (t m j) -> p m j t", t=PACK, j=PACK)[:, c0 // PACK : c1 // PACK]
+            copy(dst, raw.rearrange("p j (m t) -> p m j t", t=PACK))
+
+        def mx_tiles(cols, name):
+            codes = keep.tile([P, cols], U32, name=name + "_codes", align_bytes=64)
+            plane = keep.tile([P, cols], U8, name=name + "_plane", align_bytes=64)
+            return codes, plane
+
+        def quantise(tiles, c0, c1, grouped):
+            nc.vector.quantize_mx(out=tiles[0][:, c0:c1].bitcast(FP8X4), scales=tiles[1][:, c0:c1], in_=grouped)
+
+        def product(bank, stationary, moving):
+            nc.tensor.matmul_mx(
+                out=bank,
+                lhsT=stationary[0][:].bitcast(FP8X4),
+                lhsT_scale=stationary[1][:],
+                rhs=moving[0][:].bitcast(FP8X4),
+                rhs_scale=moving[1][:],
+                start=True,
+                stop=True,
+            )
+
+        x_scale_table = clear_scales(T, "x_scale_table")
+
+        e_word_table = load_words(e_words, W, "e_word_table")
+        mds_list = load_list(mds, "mds_list")
+        e_scale_table = keep.tile([P, W], U8, name="e_scale_table", align_bytes=64)
+        for q in range(4):
+            rows = e_scales[0, 4 * q : 4 * q + 4, :].bitcast(I32).unsqueeze(0).to_broadcast([8, 4, W // 4])
+            nc.sync.dma_start(e_scale_table[32 * q : 32 * q + 32, :].bitcast(I32), rows)
+        w2_first = load_weight(w2, 0, HALF, "w2_first")
+        w2_second = load_weight(w2, HALF, H, "w2_second")
+        offs_list = load_list(offs, "offs_list")
+        load_scales(nc.sync, x_scale_table, x_scales)
+        x_word_table = load_words(x_words, T, "x_word_table")
+        md_list = load_list(md, "md_list")
+        w1_raw = [load_weight(w1, h * HALF, (h + 1) * HALF, "w1_raw%d" % h) for h in range(2)]
+        unit_cols = keep.tile([P, PACK], F32, name="unit_cols")
+        nc.sync.dma_start(unit_cols[:], unit.rearrange("(p t) o -> p (t o)", t=PACK))
+        prv_list = load_list(prv, "prv_list")
+        w3_raw = load_weight(w3, 0, N, "w3_raw")
+
+        w2_bf = keep.tile([P, PACK * H], BF16, name="w2_bf", align_bytes=64)
+        deal(nc.scalar.copy, w2_bf, w2_first[:], 0, HALF)
+        e_codes = pick(e_word_table, mds_list, U32, "e_codes", "e_codes")
+        e_picked = (e_codes, pick(e_scale_table, mds_list, U8, "e_plane", "e_plane"))
+        deal(nc.scalar.copy, w2_bf, w2_second[:, :, 0:96], HALF, HALF + 96)
+        deal(nc.vector.tensor_copy, w2_bf, w2_second[:, :, 96:256], HALF + 96, H)
+        em = keep.tile([P, PACK, S], F32, name="em")
+        ye_banks = []
+        for t in range(PACK):
+            w2_q = mx_tiles(P, "w2_%d" % t)
+            quantise(w2_q, 0, P, w2_bf[:, t * 512 : (t + 1) * 512])
+            bank = psum.tile([P, S], F32, name="ye_bank%d" % t)
+            product(bank[:], w2_q, e_picked)
+            ye_banks.append(bank)
+        for t in range(PACK):
+            ye = keep.tile([P, S], F32, name="ye%d" % t)
+            nc.scalar.copy(ye[:], ye_banks[t][:])
+            for h in range(2):
+                cols = slice(h * HALF, (h + 1) * HALF)
+                nc.scalar.activation(em[:, t, cols], ye[:].indirect(md_list[:, h * 16 : (h + 1) * 16]), COPY)
+
+        x_plane = pick(x_scale_table, offs_list, U8, "x_plane", "w2_bf")
+        x_picked = (pick(x_word_table, offs_list, U32, "x_codes", "x_codes"), x_plane)
+        w1_bf = keep.tile([P, PACK * H], BF16, name="w1_bf", align_bytes=64)
+        w1_qs = [mx_tiles(P, "w1_%d" % t) for t in range(PACK)]
+        for h in range(2):
+            deal(nc.vector.tensor_copy, w1_bf, w1_raw[h][:], h * HALF, (h + 1) * HALF)
+            for t in range(PACK):
+                quantise(w1_qs[t], 64 * h, 64 * (h + 1), w1_bf[:, t * 512 + h * HALF : t * 512 + (h + 1) * HALF])
+        y_banks = []
+        for t in range(PACK):
+            w1_q = w1_qs[t]
+            bank = psum.tile([P, S], F32, name="y_bank%d" % t)
+            product(bank[:], w1_q, x_picked)
+            y_banks.append(bank)
+
+        w3_bf = keep.tile([P, N * PACK], BF16, name="w3_bf", align_bytes=64)
+        nc.vector.tensor_copy(
+            w3_bf[:].rearrange("p (c i j) -> p c j i", i=4, j=PACK), w3_raw[:].rearrange("p j (c i) -> p c j i", i=4)
+        )
+        w3_q = mx_tiles(N, "w3")
+        quantise(w3_q, 0, N, w3_bf[:])
+
+        res = []
+        for t in range(PACK):
+            r = keep.tile([P, S], F32, name="res%d" % t)
+            nc.vector.scalar_tensor_tensor(r[:], y_banks[t][:], unit_cols[:, t : t + 1], em[:, t, :], MULT, MULT)
+            res.append(r)
+
+        for c, (c0, c1) in enumerate(CHUNKS):
+            n = c1 - c0
+            acc = keep.tile([P, PACK, n], F32, name="acc%d" % c)
+            for t in range(PACK):
+                rp = keep.tile([P, n], F32, name="rp%d_%d" % (c, t), tag="rp%d" % t)
+                nc.scalar.activation(rp[:], res[t][:].indirect(prv_list[:, c0 // STRIPE : c1 // STRIPE]), COPY)
+                nc.vector.tensor_tensor(acc[:, t, :], rp[:], res[t][:, c0:c1], ADD)
+            hid = keep.tile([P, n * PACK], BF16, name="hid%d" % c, align_bytes=64)
+            nc.vector.tensor_tensor(
+                hid[:].rearrange("p (c i t) -> p c t i", i=4, t=PACK),
+                acc[:].rearrange("p t (c i) -> p c t i", i=4),
+                em[:, :, c0:c1].rearrange("p t (c i) -> p c t i", i=4),
+                MULT,
+            )
+            hid_q = mx_tiles(n, "hid%d" % c)
+            quantise(hid_q, 0, n, hid[:])
+            bank = psum.tile([P, S], F32, name="out_bank%d" % c, tag="ye_bank%d" % c)
+            product(bank[:, 0:n], w3_q, hid_q)
+            staged = keep.tile([P, n], F32, name="staged%d" % c)
+            nc.scalar.copy(staged[:], bank[:, 0:n])
+            nc.sync.dma_start(out[:, c0:c1], staged[:])

@@ -44,12 +44,12 @@ def tile_picked_ytransc_acc_p_kernel(tc, x_words, x_scales, w1, e_words, e_scale
             nc.vector.memset(scales[:].bitcast(I32), 0)
             return scales
 
-        def load_scales(queue, scales, src):
-            for q in range(4):
-                queue.dma_start(scales[32 * q : 32 * q + 4, :].bitcast(I32), src[0, 4 * q : 4 * q + 4, :].bitcast(I32))
+        def load_scales(scales, src):
+            for r in range(4):
+                nc.sync.dma_start(scales[r:P:32, :].bitcast(I32), src[0, r:16:4, :].bitcast(I32))
 
         def load_weight(src, c0, c1, name):
-            raw = keep.tile([P, PACK, c1 - c0], F32, name=name)
+            raw = keep.tile([P, PACK, c1 - c0], F32, name=name, align_bytes=64)
             nc.sync.dma_start(raw[:], src.rearrange("(p j) c -> p j c", j=PACK)[:, :, c0:c1])
             return raw
 
@@ -58,9 +58,10 @@ def tile_picked_ytransc_acc_p_kernel(tc, x_words, x_scales, w1, e_words, e_scale
             nc.vector.tensor_copy(picked[:], table[:].bitcast(dtype).indirect(lst[:]))
             return picked
 
-        def deal(copy, grouped, raw, c0, c1):
-            dst = grouped[:].rearrange("p (t m j) -> p m j t", t=PACK, j=PACK)[:, c0 // PACK : c1 // PACK]
-            copy(dst, raw.rearrange("p j (m t) -> p m j t", t=PACK))
+        def deal(copy, grouped, raw, c0, c1, u):
+            dst = grouped[:].rearrange("p (t m j) -> p m j t", t=PACK, j=PACK)
+            src = raw.rearrange("p j (m t) -> p m j t", t=PACK)
+            copy(dst[:, c0 // PACK : c1 // PACK, :, 2 * u : 2 * u + 2], src[:, :, :, 2 * u : 2 * u + 2])
 
         def mx_tiles(cols, name):
             codes = keep.tile([P, cols], U32, name=name + "_codes", align_bytes=64)
@@ -70,71 +71,78 @@ def tile_picked_ytransc_acc_p_kernel(tc, x_words, x_scales, w1, e_words, e_scale
         def quantise(tiles, c0, c1, grouped):
             nc.vector.quantize_mx(out=tiles[0][:, c0:c1].bitcast(FP8X4), scales=tiles[1][:, c0:c1], in_=grouped)
 
-        def product(bank, stationary, moving):
+        def product(bank, stationary, moving, c0, c1):
             nc.tensor.matmul_mx(
-                out=bank,
+                out=bank[:, c0:c1],
                 lhsT=stationary[0][:].bitcast(FP8X4),
                 lhsT_scale=stationary[1][:],
-                rhs=moving[0][:].bitcast(FP8X4),
-                rhs_scale=moving[1][:],
+                rhs=moving[0][:, c0:c1].bitcast(FP8X4),
+                rhs_scale=moving[1][:, c0:c1],
                 start=True,
                 stop=True,
             )
 
+        e_scale_table = clear_scales(W, "e_scale_table")
         x_scale_table = clear_scales(T, "x_scale_table")
 
         e_word_table = load_words(e_words, W, "e_word_table")
         mds_list = load_list(mds, "mds_list")
-        e_scale_table = keep.tile([P, W], U8, name="e_scale_table", align_bytes=64)
-        for q in range(4):
-            rows = e_scales[0, 4 * q : 4 * q + 4, :].bitcast(I32).unsqueeze(0).to_broadcast([8, 4, W // 4])
-            nc.sync.dma_start(e_scale_table[32 * q : 32 * q + 32, :].bitcast(I32), rows)
+        load_scales(e_scale_table, e_scales)
         w2_first = load_weight(w2, 0, HALF, "w2_first")
         w2_second = load_weight(w2, HALF, H, "w2_second")
         offs_list = load_list(offs, "offs_list")
-        load_scales(nc.sync, x_scale_table, x_scales)
-        x_word_table = load_words(x_words, T, "x_word_table")
         md_list = load_list(md, "md_list")
+        load_scales(x_scale_table, x_scales)
+        x_word_table = load_words(x_words, T, "x_word_table")
         w1_raw = [load_weight(w1, h * HALF, (h + 1) * HALF, "w1_raw%d" % h) for h in range(2)]
-        unit_cols = keep.tile([P, PACK], F32, name="unit_cols")
+        unit_cols = keep.tile([P, PACK], F32, name="unit_cols", tag="ring1")
         nc.sync.dma_start(unit_cols[:], unit.rearrange("(p t) o -> p (t o)", t=PACK))
         prv_list = load_list(prv, "prv_list")
         w3_raw = load_weight(w3, 0, N, "w3_raw")
 
         w2_bf = keep.tile([P, PACK * H], BF16, name="w2_bf", align_bytes=64)
-        deal(nc.scalar.copy, w2_bf, w2_first[:], 0, HALF)
+        for u in range(2):
+            deal(nc.scalar.copy, w2_bf, w2_first[:], 0, HALF, u)
         e_codes = pick(e_word_table, mds_list, U32, "e_codes", "e_codes")
         e_picked = (e_codes, pick(e_scale_table, mds_list, U8, "e_plane", "e_plane"))
-        deal(nc.scalar.copy, w2_bf, w2_second[:, :, 0:96], HALF, HALF + 96)
-        deal(nc.vector.tensor_copy, w2_bf, w2_second[:, :, 96:256], HALF + 96, H)
+        for u in range(2):
+            deal(nc.scalar.copy, w2_bf, w2_second[:, :, 0:96], HALF, HALF + 96, u)
+            deal(nc.vector.tensor_copy, w2_bf, w2_second[:, :, 96:256], HALF + 96, H, u)
         em = keep.tile([P, PACK, S], F32, name="em")
         ye_banks = []
         for t in range(PACK):
             w2_q = mx_tiles(P, "w2_%d" % t)
             quantise(w2_q, 0, P, w2_bf[:, t * 512 : (t + 1) * 512])
-            bank = psum.tile([P, S], F32, name="ye_bank%d" % t)
-            product(bank[:], w2_q, e_picked)
-            ye_banks.append(bank)
-        for t in range(PACK):
-            ye = keep.tile([P, S], F32, name="ye%d" % t)
-            nc.scalar.copy(ye[:], ye_banks[t][:])
-            for h in range(2):
-                cols = slice(h * HALF, (h + 1) * HALF)
-                nc.scalar.activation(em[:, t, cols], ye[:].indirect(md_list[:, h * 16 : (h + 1) * 16]), COPY)
+            pieces = []
+            for c0, c1 in ((0, HALF), (HALF, S)) if t == 0 else ((0, S),):
+                bank = psum.tile([P, S], F32, name="ye_bank%d_%d" % (t, c0), tag="y_bank3" if c0 else "ye_bank%d" % t)
+                product(bank, w2_q, e_picked, c0, c1)
+                pieces.append((bank, c0, c1))
+            ye_banks.append(pieces)
+        ye = [keep.tile([P, S], F32, name="ye%d" % t) for t in range(PACK)]
 
-        x_plane = pick(x_scale_table, offs_list, U8, "x_plane", "w2_bf")
+        def fetch_modes(t, h):
+            return em[:, t, h * HALF : (h + 1) * HALF], ye[t][:].indirect(md_list[:, h * 16 : (h + 1) * 16])
+
+        x_plane = pick(x_scale_table, offs_list, U8, "x_plane", "w2_second")
+        for t in range(PACK):
+            for bank, c0, c1 in ye_banks[t]:
+                nc.scalar.copy(ye[t][:, c0:c1], bank[:, c0:c1])
+            for h in range(2):
+                nc.scalar.activation(*fetch_modes(t, h), COPY)
+
         x_picked = (pick(x_word_table, offs_list, U32, "x_codes", "x_codes"), x_plane)
         w1_bf = keep.tile([P, PACK * H], BF16, name="w1_bf", align_bytes=64)
         w1_qs = [mx_tiles(P, "w1_%d" % t) for t in range(PACK)]
         for h in range(2):
-            deal(nc.vector.tensor_copy, w1_bf, w1_raw[h][:], h * HALF, (h + 1) * HALF)
+            for u in range(2):
+                deal(nc.vector.tensor_copy, w1_bf, w1_raw[h][:], h * HALF, (h + 1) * HALF, u)
             for t in range(PACK):
                 quantise(w1_qs[t], 64 * h, 64 * (h + 1), w1_bf[:, t * 512 + h * HALF : t * 512 + (h + 1) * HALF])
         y_banks = []
         for t in range(PACK):
-            w1_q = w1_qs[t]
             bank = psum.tile([P, S], F32, name="y_bank%d" % t)
-            product(bank[:], w1_q, x_picked)
+            product(bank, w1_qs[t], x_picked, 0, S)
             y_banks.append(bank)
 
         w3_bf = keep.tile([P, N * PACK], BF16, name="w3_bf", align_bytes=64)
@@ -142,32 +150,42 @@ def tile_picked_ytransc_acc_p_kernel(tc, x_words, x_scales, w1, e_words, e_scale
             w3_bf[:].rearrange("p (c i j) -> p c j i", i=4, j=PACK), w3_raw[:].rearrange("p j (c i) -> p c j i", i=4)
         )
         w3_q = mx_tiles(N, "w3")
+
+        res = keep.tile([P, PACK, S], F32, name="res")
+        for t in range(PACK):
+            nc.vector.scalar_tensor_tensor(res[:, t, :], y_banks[t][:], unit_cols[:, t : t + 1], em[:, t, :], MULT, MULT)
         quantise(w3_q, 0, N, w3_bf[:])
 
-        res = []
-        for t in range(PACK):
-            r = keep.tile([P, S], F32, name="res%d" % t)
-            nc.vector.scalar_tensor_tensor(r[:], y_banks[t][:], unit_cols[:, t : t + 1], em[:, t, :], MULT, MULT)
-            res.append(r)
-
+        out_banks = [psum.tile([P, S], F32, name="out_bank%d" % b, tag="ye_bank%d" % b) for b in range(2)]
+        last = len(CHUNKS) - 1
         for c, (c0, c1) in enumerate(CHUNKS):
             n = c1 - c0
-            acc = keep.tile([P, PACK, n], F32, name="acc%d" % c)
-            for t in range(PACK):
-                rp = keep.tile([P, n], F32, name="rp%d_%d" % (c, t), tag="rp%d" % t)
-                nc.scalar.activation(rp[:], res[t][:].indirect(prv_list[:, c0 // STRIPE : c1 // STRIPE]), COPY)
-                nc.vector.tensor_tensor(acc[:, t, :], rp[:], res[t][:, c0:c1], ADD)
+            acc = keep.tile([P, PACK, n], F32, name="acc%d" % c, tag=("ring3", "ring0b", "ring1", "ring0")[c])
+            for t0, t1 in ((0, 3), (3, 4)) if c == 0 else ((0, 4),):
+                tag = "ring0b" if t0 else ("ring0", "ring1", "ring0", "ring3")[c]
+                rp = keep.tile([P, t1 - t0, n], F32, name="rp%d_%d" % (c, t0), tag=tag)
+                for t in range(t0, t1):
+                    nc.scalar.activation(rp[:, t - t0, :], res[:, t, :].indirect(prv_list[:, c0 // STRIPE : c1 // STRIPE]), COPY)
+                nc.vector.tensor_tensor(acc[:, t0:t1, :], rp[:], res[:, t0:t1, c0:c1], ADD)
             hid = keep.tile([P, n * PACK], BF16, name="hid%d" % c, align_bytes=64)
             nc.vector.tensor_tensor(
-                hid[:].rearrange("p (c i t) -> p c t i", i=4, t=PACK),
-                acc[:].rearrange("p t (c i) -> p c t i", i=4),
-                em[:, :, c0:c1].rearrange("p t (c i) -> p c t i", i=4),
+                hid[:].rearrange("p (c i t) -> p c t i", i=2, t=PACK),
+                acc[:].rearrange("p t (c i) -> p c t i", i=2),
+                em[:, :, c0:c1].rearrange("p t (c i) -> p c t i", i=2),
                 MULT,
             )
             hid_q = mx_tiles(n, "hid%d" % c)
             quantise(hid_q, 0, n, hid[:])
-            bank = psum.tile([P, S], F32, name="out_bank%d" % c, tag="ye_bank%d" % c)
-            product(bank[:, 0:n], w3_q, hid_q)
-            staged = keep.tile([P, n], F32, name="staged%d" % c)
-            nc.scalar.copy(staged[:], bank[:, 0:n])
-            nc.sync.dma_start(out[:, c0:c1], staged[:])
+            nc.tensor.matmul_mx(
+                out=out_banks[c // last][:, c0:c1],
+                lhsT=w3_q[0][:].bitcast(FP8X4),
+                lhsT_scale=w3_q[1][:],
+                rhs=hid_q[0][:].bitcast(FP8X4),
+                rhs_scale=hid_q[1][:],
+                start=True,
+                stop=True,
+            )
+        staged = keep.tile([P, S], F32, name="staged", tag="res")
+        for b, (c0, c1) in enumerate(((0, CHUNKS[last][0]), CHUNKS[last])):
+            nc.scalar.copy(staged[:, c0:c1], out_banks[b][:, c0:c1])
+            nc.sync.dma_start(out[:, c0:c1], staged[:, c0:c1])

@@ -19,61 +19,69 @@ COPY = mybir.ActivationFunctionType.Copy
 P = 128
 PACK = 4
 STRIPE = 16
+QUADRANT = 32
 HALF = S // 2
-CHUNKS = ((0, 128), (128, 256), (256, 384), (384, 512))
+W1_PIECES = ((0, 256), (256, 384), (384, 512))
+W2_SCALAR_COLS = 96
+CHUNK = 128
+CHUNKS = S // CHUNK
 
 
-def tile_picked_ytransc_acc_p_kernel(tc, x_words, x_scales, w1, e_words, e_scales, w2, unit, w3, offs, mds, md, prv, out):
+def tile_picked_ytransc_acc_p_kernel(
+    tc, x_words, x_scales, w1, e_words, e_scales, w2, unit, w3, offs, mds, md, prv, out
+):
     nc = tc.nc
     with ExitStack() as ctx:
         keep = ctx.enter_context(tc.tile_pool(name="keep", bufs=1))
         psum = ctx.enter_context(tc.psum_pool(name="psum", bufs=1))
 
         def load_list(src, name):
-            lst = keep.tile([P, S // STRIPE], U16, name=name)
-            nc.sync.dma_start(lst[:], src)
-            return lst
+            entries = keep.tile([P, S // STRIPE], U16, name=name)
+            nc.sync.dma_start(entries[:], src)
+            return entries
 
         def load_words(src, cols, name):
             words = keep.tile([P, cols], I32, name=name, align_bytes=64)
             nc.sync.dma_start(words[:], src[0].rearrange("p n t -> p (n t)").bitcast(I32))
             return words
 
-        def clear_scales(cols, name):
-            scales = keep.tile([P, cols], U8, name=name, align_bytes=64)
-            nc.vector.memset(scales[:].bitcast(I32), 0)
-            return scales
+        def zeroed_scale_table(cols, name):
+            table = keep.tile([P, cols], U8, name=name, align_bytes=64)
+            nc.vector.memset(table[:].bitcast(I32), 0)
+            return table
 
-        def load_scales(scales, src):
-            for r in range(4):
-                nc.sync.dma_start(scales[r:P:32, :].bitcast(I32), src[0, r:16:4, :].bitcast(I32))
+        def load_scales(table, src):
+            for r in range(PACK):
+                nc.sync.dma_start(table[r:P:QUADRANT, :].bitcast(I32), src[0, r : K // 32 : PACK, :].bitcast(I32))
 
         def load_weight(src, c0, c1, name):
             raw = keep.tile([P, PACK, c1 - c0], F32, name=name, align_bytes=64)
             nc.sync.dma_start(raw[:], src.rearrange("(p j) c -> p j c", j=PACK)[:, :, c0:c1])
             return raw
 
-        def pick(table, lst, dtype, name, tag):
+        def pick(table, entries, dtype, name, tag):
             picked = keep.tile([P, S], dtype, name=name, tag=tag, align_bytes=64)
-            nc.vector.tensor_copy(picked[:], table[:].bitcast(dtype).indirect(lst[:]))
+            nc.vector.tensor_copy(picked[:], table[:].bitcast(dtype).indirect(entries[:]))
             return picked
 
-        def deal(copy, grouped, raw, c0, c1, u):
+        def deal(copy, grouped, raw, c0, c1, pair):
+            planes = slice(2 * pair, 2 * pair + 2)
             dst = grouped[:].rearrange("p (t m j) -> p m j t", t=PACK, j=PACK)
             src = raw.rearrange("p j (m t) -> p m j t", t=PACK)
-            copy(dst[:, c0 // PACK : c1 // PACK, :, 2 * u : 2 * u + 2], src[:, :, :, 2 * u : 2 * u + 2])
+            copy(dst[:, c0 // PACK : c1 // PACK, :, planes], src[:, :, :, planes])
 
         def mx_tiles(cols, name):
             codes = keep.tile([P, cols], U32, name=name + "_codes", align_bytes=64)
-            plane = keep.tile([P, cols], U8, name=name + "_plane", align_bytes=64)
-            return codes, plane
+            scales = keep.tile([P, cols], U8, name=name + "_scales", align_bytes=64)
+            return codes, scales
 
-        def quantise(tiles, c0, c1, grouped):
-            nc.vector.quantize_mx(out=tiles[0][:, c0:c1].bitcast(FP8X4), scales=tiles[1][:, c0:c1], in_=grouped)
+        def quantise(operand, c0, c1, grouped):
+            codes, scales = operand
+            nc.vector.quantize_mx(out=codes[:, c0:c1].bitcast(FP8X4), scales=scales[:, c0:c1], in_=grouped)
 
-        def product(bank, stationary, moving, c0, c1):
+        def product(target, stationary, moving, c0, c1):
             nc.tensor.matmul_mx(
-                out=bank[:, c0:c1],
+                out=target,
                 lhsT=stationary[0][:].bitcast(FP8X4),
                 lhsT_scale=stationary[1][:],
                 rhs=moving[0][:, c0:c1].bitcast(FP8X4),
@@ -82,8 +90,8 @@ def tile_picked_ytransc_acc_p_kernel(tc, x_words, x_scales, w1, e_words, e_scale
                 stop=True,
             )
 
-        e_scale_table = clear_scales(W, "e_scale_table")
-        x_scale_table = clear_scales(T, "x_scale_table")
+        e_scale_table = zeroed_scale_table(W, "e_scale_table")
+        x_scale_table = zeroed_scale_table(T, "x_scale_table")
 
         e_word_table = load_words(e_words, W, "e_word_table")
         mds_list = load_list(mds, "mds_list")
@@ -94,98 +102,106 @@ def tile_picked_ytransc_acc_p_kernel(tc, x_words, x_scales, w1, e_words, e_scale
         md_list = load_list(md, "md_list")
         load_scales(x_scale_table, x_scales)
         x_word_table = load_words(x_words, T, "x_word_table")
-        w1_raw = [load_weight(w1, h * HALF, (h + 1) * HALF, "w1_raw%d" % h) for h in range(2)]
-        unit_cols = keep.tile([P, PACK], F32, name="unit_cols", tag="ring1")
+        w1_raw = [load_weight(w1, c0, c1, "w1_raw%d" % c0) for c0, c1 in W1_PIECES]
+        unit_cols = keep.tile([P, PACK], F32, name="unit_cols", tag="slot_b")
         nc.sync.dma_start(unit_cols[:], unit.rearrange("(p t) o -> p (t o)", t=PACK))
         prv_list = load_list(prv, "prv_list")
         w3_raw = load_weight(w3, 0, N, "w3_raw")
 
         w2_bf = keep.tile([P, PACK * H], BF16, name="w2_bf", align_bytes=64)
-        for u in range(2):
-            deal(nc.scalar.copy, w2_bf, w2_first[:], 0, HALF, u)
+        for pair in range(2):
+            deal(nc.scalar.copy, w2_bf, w2_first[:], 0, HALF, pair)
         e_codes = pick(e_word_table, mds_list, U32, "e_codes", "e_codes")
-        e_picked = (e_codes, pick(e_scale_table, mds_list, U8, "e_plane", "e_plane"))
-        for u in range(2):
-            deal(nc.scalar.copy, w2_bf, w2_second[:, :, 0:96], HALF, HALF + 96, u)
-            deal(nc.vector.tensor_copy, w2_bf, w2_second[:, :, 96:256], HALF + 96, H, u)
+        e_picked = (e_codes, pick(e_scale_table, mds_list, U8, "e_picked_scales", "e_picked_scales"))
+        border = HALF + W2_SCALAR_COLS
+        for pair in range(2):
+            deal(nc.scalar.copy, w2_bf, w2_second[:, :, 0:W2_SCALAR_COLS], HALF, border, pair)
+            deal(nc.vector.tensor_copy, w2_bf, w2_second[:, :, W2_SCALAR_COLS:HALF], border, H, pair)
         em = keep.tile([P, PACK, S], F32, name="em")
         ye_banks = []
         for t in range(PACK):
-            w2_q = mx_tiles(P, "w2_%d" % t)
-            quantise(w2_q, 0, P, w2_bf[:, t * 512 : (t + 1) * 512])
+            w2_plane = mx_tiles(P, "w2_%d" % t)
+            quantise(w2_plane, 0, P, w2_bf[:, t * H : (t + 1) * H])
             pieces = []
             for c0, c1 in ((0, HALF), (HALF, S)) if t == 0 else ((0, S),):
                 bank = psum.tile([P, S], F32, name="ye_bank%d_%d" % (t, c0), tag="y_bank3" if c0 else "ye_bank%d" % t)
-                product(bank, w2_q, e_picked, c0, c1)
+                product(bank[:, c0:c1], w2_plane, e_picked, c0, c1)
                 pieces.append((bank, c0, c1))
             ye_banks.append(pieces)
         ye = [keep.tile([P, S], F32, name="ye%d" % t) for t in range(PACK)]
 
-        def fetch_modes(t, h):
-            return em[:, t, h * HALF : (h + 1) * HALF], ye[t][:].indirect(md_list[:, h * 16 : (h + 1) * 16])
+        x_picked_scales = pick(x_scale_table, offs_list, U8, "x_picked_scales", "w2_second")
 
-        x_plane = pick(x_scale_table, offs_list, U8, "x_plane", "w2_second")
         for t in range(PACK):
             for bank, c0, c1 in ye_banks[t]:
                 nc.scalar.copy(ye[t][:, c0:c1], bank[:, c0:c1])
-            for h in range(2):
-                nc.scalar.activation(*fetch_modes(t, h), COPY)
+            for c0 in (0, HALF):
+                entries = md_list[:, c0 // STRIPE : (c0 + HALF) // STRIPE]
+                nc.scalar.activation(em[:, t, c0 : c0 + HALF], ye[t][:].indirect(entries), COPY)
 
-        x_picked = (pick(x_word_table, offs_list, U32, "x_codes", "x_codes"), x_plane)
+        x_picked = (pick(x_word_table, offs_list, U32, "x_codes", "x_codes"), x_picked_scales)
         w1_bf = keep.tile([P, PACK * H], BF16, name="w1_bf", align_bytes=64)
-        w1_qs = [mx_tiles(P, "w1_%d" % t) for t in range(PACK)]
-        for h in range(2):
-            for u in range(2):
-                deal(nc.vector.tensor_copy, w1_bf, w1_raw[h][:], h * HALF, (h + 1) * HALF, u)
+        w1_planes = [mx_tiles(P, "w1_%d" % t) for t in range(PACK)]
+        for half in range(2):
+            for raw, (c0, c1) in zip(w1_raw, W1_PIECES):
+                if c0 // HALF == half:
+                    for pair in range(2):
+                        deal(nc.vector.tensor_copy, w1_bf, raw[:], c0, c1, pair)
             for t in range(PACK):
-                quantise(w1_qs[t], 64 * h, 64 * (h + 1), w1_bf[:, t * 512 + h * HALF : t * 512 + (h + 1) * HALF])
+                first = t * H + half * HALF
+                quantise(w1_planes[t], half * P // 2, (half + 1) * P // 2, w1_bf[:, first : first + HALF])
         y_banks = []
         for t in range(PACK):
             bank = psum.tile([P, S], F32, name="y_bank%d" % t)
-            product(bank, w1_qs[t], x_picked, 0, S)
+            product(bank[:], w1_planes[t], x_picked, 0, S)
             y_banks.append(bank)
 
         w3_bf = keep.tile([P, N * PACK], BF16, name="w3_bf", align_bytes=64)
         nc.vector.tensor_copy(
             w3_bf[:].rearrange("p (c i j) -> p c j i", i=4, j=PACK), w3_raw[:].rearrange("p j (c i) -> p c j i", i=4)
         )
-        w3_q = mx_tiles(N, "w3")
+        w3_mx = mx_tiles(N, "w3")
 
         res = keep.tile([P, PACK, S], F32, name="res")
         for t in range(PACK):
             nc.vector.scalar_tensor_tensor(res[:, t, :], y_banks[t][:], unit_cols[:, t : t + 1], em[:, t, :], MULT, MULT)
-        quantise(w3_q, 0, N, w3_bf[:])
+        quantise(w3_mx, 0, N, w3_bf[:])
 
-        out_banks = [psum.tile([P, S], F32, name="out_bank%d" % b, tag="ye_bank%d" % b) for b in range(2)]
-        last = len(CHUNKS) - 1
-        for c, (c0, c1) in enumerate(CHUNKS):
-            n = c1 - c0
-            acc = keep.tile([P, PACK, n], F32, name="acc%d" % c, tag=("ring3", "ring0b", "ring1", "ring0")[c])
-            for t0, t1 in ((0, 3), (3, 4)) if c == 0 else ((0, 4),):
-                tag = "ring0b" if t0 else ("ring0", "ring1", "ring0", "ring3")[c]
-                rp = keep.tile([P, t1 - t0, n], F32, name="rp%d_%d" % (c, t0), tag=tag)
+        fetched_slots = ("slot_a", "slot_b", "slot_a", "slot_c")
+        acc_slots = ("slot_c", "slot_d", "slot_b", "slot_a")
+        last = CHUNKS - 1
+        early_bank = psum.tile([P, S], F32, name="early_bank", tag="ye_bank0")
+        results = [(early_bank, 0, last * CHUNK)]
+        for c in range(CHUNKS):
+            c0, c1 = c * CHUNK, (c + 1) * CHUNK
+            entries = prv_list[:, c0 // STRIPE : c1 // STRIPE]
+            acc = keep.tile([P, PACK, CHUNK], F32, name="acc%d" % c, tag=acc_slots[c])
+            for t0, t1 in ((0, PACK - 1), (PACK - 1, PACK)) if c == 0 else ((0, PACK),):
+                slot = "slot_d" if t0 else fetched_slots[c]
+                fetched = keep.tile([P, t1 - t0, CHUNK], F32, name="fetched%d_%d" % (c, t0), tag=slot)
                 for t in range(t0, t1):
-                    nc.scalar.activation(rp[:, t - t0, :], res[:, t, :].indirect(prv_list[:, c0 // STRIPE : c1 // STRIPE]), COPY)
-                nc.vector.tensor_tensor(acc[:, t0:t1, :], rp[:], res[:, t0:t1, c0:c1], ADD)
-            hid = keep.tile([P, n * PACK], BF16, name="hid%d" % c, align_bytes=64)
-            nc.vector.tensor_tensor(
-                hid[:].rearrange("p (c i t) -> p c t i", i=2, t=PACK),
-                acc[:].rearrange("p t (c i) -> p c t i", i=2),
-                em[:, :, c0:c1].rearrange("p t (c i) -> p c t i", i=2),
-                MULT,
-            )
-            hid_q = mx_tiles(n, "hid%d" % c)
-            quantise(hid_q, 0, n, hid[:])
-            nc.tensor.matmul_mx(
-                out=out_banks[c // last][:, c0:c1],
-                lhsT=w3_q[0][:].bitcast(FP8X4),
-                lhsT_scale=w3_q[1][:],
-                rhs=hid_q[0][:].bitcast(FP8X4),
-                rhs_scale=hid_q[1][:],
-                start=True,
-                stop=True,
-            )
+                    nc.scalar.activation(fetched[:, t - t0, :], res[:, t, :].indirect(entries), COPY)
+                nc.vector.tensor_tensor(acc[:, t0:t1, :], fetched[:], res[:, t0:t1, c0:c1], ADD)
+            for p0, p1 in ((0, CHUNK // 2), (CHUNK // 2, CHUNK)) if c == last else ((0, CHUNK),):
+                hid = keep.tile([P, (p1 - p0) * PACK], BF16, name="hid%d_%d" % (c, p0), align_bytes=64)
+                nc.vector.tensor_tensor(
+                    hid[:].rearrange("p (c i t) -> p c t i", i=2, t=PACK),
+                    acc[:, :, p0:p1].rearrange("p t (c i) -> p c t i", i=2),
+                    em[:, :, c0 + p0 : c0 + p1].rearrange("p t (c i) -> p c t i", i=2),
+                    MULT,
+                )
+                hid_mx = mx_tiles(p1 - p0, "hid%d_%d" % (c, p0))
+                quantise(hid_mx, 0, p1 - p0, hid[:])
+                if c == last:
+                    bank = psum.tile([P, S], F32, name="late_bank%d" % p0, tag="ye_bank2" if p0 else "ye_bank1")
+                    target = bank[:, 0 : p1 - p0]
+                    results.append((bank, c0 + p0, c0 + p1))
+                else:
+                    target = early_bank[:, c0:c1]
+                product(target, w3_mx, hid_mx, 0, p1 - p0)
+
         staged = keep.tile([P, S], F32, name="staged", tag="res")
-        for b, (c0, c1) in enumerate(((0, CHUNKS[last][0]), CHUNKS[last])):
-            nc.scalar.copy(staged[:, c0:c1], out_banks[b][:, c0:c1])
+        for bank, c0, c1 in results:
+            nc.scalar.copy(staged[:, c0:c1], bank[:, 0 : c1 - c0])
+        for c0, c1 in ((0, last * CHUNK), (last * CHUNK, S)):
             nc.sync.dma_start(out[:, c0:c1], staged[:, c0:c1])

from contextlib import ExitStack

import concourse.mybir as mybir

K, T, S, N, H, W = 512, 2048, 512, 128, 512, 1024
FLOPS = 2 * K * H * S * 2 + 2 * H * N * S

F32 = mybir.dt.float32
BF16 = mybir.dt.bfloat16
I32 = mybir.dt.int32
U32 = mybir.dt.uint32
U16 = mybir.dt.uint16
U8 = mybir.dt.uint8
FP8X4 = mybir.dt.float8_e4m3fn_x4
MULT = mybir.AluOpType.mult
ADD = mybir.AluOpType.add
COPY = mybir.ActivationFunctionType.Copy

P = 128
PACK = 4
STRIPE = 16
QUADRANT = 32
HALF = S // 2
W1_PIECES = ((0, 256), (256, 384), (384, 512))
W2_SCALAR_COLS = 96
CHUNK = 128
CHUNKS = S // CHUNK


def tile_picked_ytransc_acc_p_kernel(
    tc, x_words, x_scales, w1, e_words, e_scales, w2, unit, w3, offs, mds, md, prv, out
):
    nc = tc.nc
    with ExitStack() as ctx:
        keep = ctx.enter_context(tc.tile_pool(name="keep", bufs=1))
        psum = ctx.enter_context(tc.psum_pool(name="psum", bufs=1))

        def load_list(src, name):
            entries = keep.tile([P, S // STRIPE], U16, name=name)
            nc.sync.dma_start(entries[:], src)
            return entries

        def load_words(src, cols, name):
            words = keep.tile([P, cols], I32, name=name, align_bytes=64)
            nc.sync.dma_start(words[:], src[0].rearrange("p n t -> p (n t)").bitcast(I32))
            return words

        def zeroed_scale_table(cols, name):
            table = keep.tile([P, cols], U8, name=name, align_bytes=64)
            nc.vector.memset(table[:].bitcast(I32), 0)
            return table

        def load_scales(table, src):
            for r in range(PACK):
                nc.sync.dma_start(table[r:P:QUADRANT, :].bitcast(I32), src[0, r : K // 32 : PACK, :].bitcast(I32))

        def load_weight(src, c0, c1, name):
            raw = keep.tile([P, PACK, c1 - c0], F32, name=name, align_bytes=64)
            nc.sync.dma_start(raw[:], src.rearrange("(p j) c -> p j c", j=PACK)[:, :, c0:c1])
            return raw

        def pick(table, entries, dtype, name, tag):
            picked = keep.tile([P, S], dtype, name=name, tag=tag, align_bytes=64)
            nc.vector.tensor_copy(picked[:], table[:].bitcast(dtype).indirect(entries[:]))
            return picked

        def deal(copy, grouped, raw, c0, c1, pair):
            planes = slice(2 * pair, 2 * pair + 2)
            dst = grouped[:].rearrange("p (t m j) -> p m j t", t=PACK, j=PACK)
            src = raw.rearrange("p j (m t) -> p m j t", t=PACK)
            copy(dst[:, c0 // PACK : c1 // PACK, :, planes], src[:, :, :, planes])

        def mx_tiles(cols, name):
            codes = keep.tile([P, cols], U32, name=name + "_codes", align_bytes=64)
            scales = keep.tile([P, cols], U8, name=name + "_scales", align_bytes=64)
            return codes, scales

        def quantise(operand, c0, c1, grouped):
            codes, scales = operand
            nc.vector.quantize_mx(out=codes[:, c0:c1].bitcast(FP8X4), scales=scales[:, c0:c1], in_=grouped)

        def product(target, stationary, moving, c0, c1):
            nc.tensor.matmul_mx(
                out=target,
                lhsT=stationary[0][:].bitcast(FP8X4),
                lhsT_scale=stationary[1][:],
                rhs=moving[0][:, c0:c1].bitcast(FP8X4),
                rhs_scale=moving[1][:, c0:c1],
                start=True,
                stop=True,
            )

        e_scale_table = zeroed_scale_table(W, "e_scale_table")
        x_scale_table = zeroed_scale_table(T, "x_scale_table")

        e_word_table = load_words(e_words, W, "e_word_table")
        mds_list = load_list(mds, "mds_list")
        load_scales(e_scale_table, e_scales)
        w2_first = load_weight(w2, 0, HALF, "w2_first")
        w2_second = load_weight(w2, HALF, H, "w2_second")
        offs_list = load_list(offs, "offs_list")
        md_list = load_list(md, "md_list")
        load_scales(x_scale_table, x_scales)
        x_word_table = load_words(x_words, T, "x_word_table")
        w1_raw = [load_weight(w1, c0, c1, "w1_raw%d" % c0) for c0, c1 in W1_PIECES]
        unit_cols = keep.tile([P, PACK], F32, name="unit_cols", tag="slot_b")
        nc.sync.dma_start(unit_cols[:], unit.rearrange("(p t) o -> p (t o)", t=PACK))
        prv_list = load_list(prv, "prv_list")
        w3_raw = load_weight(w3, 0, N, "w3_raw")

        w2_bf = keep.tile([P, PACK * H], BF16, name="w2_bf", align_bytes=64)
        for pair in range(2):
            deal(nc.scalar.copy, w2_bf, w2_first[:], 0, HALF, pair)
        e_codes = pick(e_word_table, mds_list, U32, "e_codes", "e_codes")
        e_picked = (e_codes, pick(e_scale_table, mds_list, U8, "e_picked_scales", "e_picked_scales"))
        border = HALF + W2_SCALAR_COLS
        for pair in range(2):
            deal(nc.scalar.copy, w2_bf, w2_second[:, :, 0:W2_SCALAR_COLS], HALF, border, pair)
            deal(nc.vector.tensor_copy, w2_bf, w2_second[:, :, W2_SCALAR_COLS:HALF], border, H, pair)
        em = keep.tile([P, PACK, S], F32, name="em")
        ye_banks = []
        for t in range(PACK):
            w2_plane = mx_tiles(P, "w2_%d" % t)
            quantise(w2_plane, 0, P, w2_bf[:, t * H : (t + 1) * H])
            pieces = []
            for c0, c1 in ((0, HALF), (HALF, S)) if t == 0 else ((0, S),):
                bank = psum.tile([P, S], F32, name="ye_bank%d_%d" % (t, c0), tag="y_bank3" if c0 else "ye_bank%d" % t)
                product(bank[:, c0:c1], w2_plane, e_picked, c0, c1)
                pieces.append((bank, c0, c1))
            ye_banks.append(pieces)
        ye = [keep.tile([P, S], F32, name="ye%d" % t) for t in range(PACK)]

        x_picked_scales = pick(x_scale_table, offs_list, U8, "x_picked_scales", "w2_second")

        for t in range(PACK):
            for bank, c0, c1 in ye_banks[t]:
                nc.scalar.copy(ye[t][:, c0:c1], bank[:, c0:c1])
            for c0 in (0, HALF):
                entries = md_list[:, c0 // STRIPE : (c0 + HALF) // STRIPE]
                nc.scalar.activation(em[:, t, c0 : c0 + HALF], ye[t][:].indirect(entries), COPY)

        x_picked = (pick(x_word_table, offs_list, U32, "x_codes", "x_codes"), x_picked_scales)
        w1_bf = keep.tile([P, PACK * H], BF16, name="w1_bf", align_bytes=64)
        w1_planes = [mx_tiles(P, "w1_%d" % t) for t in range(PACK)]
        for half in range(2):
            for raw, (c0, c1) in zip(w1_raw, W1_PIECES):
                if c0 // HALF == half:
                    for pair in range(2):
                        deal(nc.vector.tensor_copy, w1_bf, raw[:], c0, c1, pair)
            for t in range(PACK):
                first = t * H + half * HALF
                quantise(w1_planes[t], half * P // 2, (half + 1) * P // 2, w1_bf[:, first : first + HALF])
        y_banks = []
        for t in range(PACK):
            bank = psum.tile([P, S], F32, name="y_bank%d" % t)
            product(bank[:], w1_planes[t], x_picked, 0, S)
            y_banks.append(bank)

        w3_bf = keep.tile([P, N * PACK], BF16, name="w3_bf", align_bytes=64)
        nc.vector.tensor_copy(
            w3_bf[:].rearrange("p (c i j) -> p c j i", i=4, j=PACK), w3_raw[:].rearrange("p j (c i) -> p c j i", i=4)
        )
        w3_mx = mx_tiles(N, "w3")

        res = keep.tile([P, PACK, S], F32, name="res")
        for t in range(PACK):
            nc.vector.scalar_tensor_tensor(res[:, t, :], y_banks[t][:], unit_cols[:, t : t + 1], em[:, t, :], MULT, MULT)
        quantise(w3_mx, 0, N, w3_bf[:])

        fetched_slots = ("slot_a", "slot_b", "slot_a", "slot_c")
        acc_slots = ("slot_c", "slot_d", "slot_b", "slot_a")
        last = CHUNKS - 1
        early_bank = psum.tile([P, S], F32, name="early_bank", tag="ye_bank0")
        results = [(early_bank, 0, last * CHUNK)]
        for c in range(CHUNKS):
            c0, c1 = c * CHUNK, (c + 1) * CHUNK
            entries = prv_list[:, c0 // STRIPE : c1 // STRIPE]
            acc = keep.tile([P, PACK, CHUNK], F32, name="acc%d" % c, tag=acc_slots[c])
            for t0, t1 in ((0, PACK - 1), (PACK - 1, PACK)) if c == 0 else ((0, PACK),):
                slot = "slot_d" if t0 else fetched_slots[c]
                fetched = keep.tile([P, t1 - t0, CHUNK], F32, name="fetched%d_%d" % (c, t0), tag=slot)
                for t in range(t0, t1):
                    nc.scalar.activation(fetched[:, t - t0, :], res[:, t, :].indirect(entries), COPY)
                nc.vector.tensor_tensor(acc[:, t0:t1, :], fetched[:], res[:, t0:t1, c0:c1], ADD)
            for p0, p1 in ((0, CHUNK // 2), (CHUNK // 2, CHUNK)) if c == last else ((0, CHUNK),):
                hid = keep.tile([P, (p1 - p0) * PACK], BF16, name="hid%d_%d" % (c, p0), align_bytes=64)
                nc.vector.tensor_tensor(
                    hid[:].rearrange("p (c i t) -> p c t i", i=2, t=PACK),
                    acc[:, :, p0:p1].rearrange("p t (c i) -> p c t i", i=2),
                    em[:, :, c0 + p0 : c0 + p1].rearrange("p t (c i) -> p c t i", i=2),
                    MULT,
                )
                hid_mx = mx_tiles(p1 - p0, "hid%d_%d" % (c, p0))
                quantise(hid_mx, 0, p1 - p0, hid[:])
                if c == last:
                    bank = psum.tile([P, S], F32, name="late_bank%d" % p0, tag="ye_bank2" if p0 else "ye_bank1")
                    target = bank[:, 0 : p1 - p0]
                    results.append((bank, c0 + p0, c0 + p1))
                else:
                    target = early_bank[:, c0:c1]
                product(target, w3_mx, hid_mx, 0, p1 - p0)

        staged = keep.tile([P, S], F32, name="staged", tag="res")
        for bank, c0, c1 in results:
            nc.scalar.copy(staged[:, c0:c1], bank[:, 0 : c1 - c0])
        for c0, c1 in ((0, last * CHUNK), (last * CHUNK, S)):
            nc.sync.dma_start(out[:, c0:c1], staged[:, c0:c1])
